import numpy as np, ml_dtypes
CORES = [32,40,48,56,64,72,80,88,96,104,112,120]
N = 12
R = 16
def setup_inputs(rng):
    m = (rng.standard_normal((N, 128, 128), dtype=np.float32) / 11).astype(ml_dtypes.bfloat16)
    q = rng.standard_normal((128, R), dtype=np.float32).astype(ml_dtypes.bfloat16)
    return {"m": m, "mt": m.transpose(0, 2, 1).copy(), "q": np.broadcast_to(q, (N, 128, R)).copy()}
def setup_inputs_big(rng):
    d = setup_inputs(rng)
    for k in ("m", "mt", "q"): d[k] = (d[k].astype(np.float32) * 1024.0).astype(d[k].dtype)
    return d
def setup_inputs_small(rng):
    d = setup_inputs(rng)
    for k in ("m", "mt", "q"): d[k] = (d[k].astype(np.float32) * (1 / 1024.0)).astype(d[k].dtype)
    return d
def setup_inputs_apart(rng):
    d = setup_inputs(rng)
    f = (10.0 ** rng.permutation(np.linspace(-1.5, 1.5, N))).astype(np.float32).reshape(N, 1, 1)
    for k in ("m", "mt"): d[k] = (d[k].astype(np.float32) * f).astype(d[k].dtype)
    return d
def reference(m, mt, q):
    M, MT, Q = m.astype(np.float64), mt.astype(np.float64), q.astype(np.float64)
    p = sum(MT[j].T @ Q[j] for j in range(N))
    q2 = sum(M[j].T @ p for j in range(N))
    return {"p": np.broadcast_to(p.astype(ml_dtypes.bfloat16), (N, 128, R)), "q2": np.broadcast_to(q2.astype(ml_dtypes.bfloat16), (N, 128, R))}

@@ -1,0 +1,139 @@
+from concourse.bass import DstId, RemoteDMATransfer
+from concourse.mybir import AluOpType
+
+D = 128
+R = 16
+W = D + R
+PLANE = 6
+GROUP_SIZES = (4, 4, 4)
+ENGINES = 8
+
+SCRATCH = {
+    "mt_s": ("sbuf", [D, D], "bfloat16"),
+    "q_s": ("sbuf", [D, R], "bfloat16"),
+    "x": ("sbuf", [D, W], "bfloat16"),
+    "red": ("sbuf", [D, PLANE * W], "bfloat16"),
+    "la": ("sbuf", [D, W], "bfloat16"),
+    "lb": ("sbuf", [D, W], "bfloat16"),
+    "p_o": ("sbuf", [D, R], "bfloat16"),
+    "q2_o": ("sbuf", [D, R], "bfloat16"),
+    "ps_p": ("psum", [D, 512], "float32"),
+    "ps_q2": ("psum", [D, 512], "float32"),
+}
+SEMAPHORES = ["ld_a", "ld_b", "mm1", "xr", "arr", "sent", "mm2", "p_r", "q2_r", "st"]
+
+
+def _pick(mask, n, skip=0):
+    bits = [b for b in range(mask.bit_length()) if (mask >> b) & 1]
+    out = 0
+    for b in bits[skip:skip + n]:
+        out |= 1 << b
+    return out
+
+
+def _common_mask(topo, src, dsts):
+    m = topo.mask(src, dsts[0])
+    for d in dsts[1:]:
+        m &= topo.mask(src, d)
+    return m
+
+
+def _plan(T, topo):
+    ranks = list(T.cores)
+    c0 = topo.chip(ranks[0])
+    pa = [c for c in ranks if topo.chip(c) == c0 or topo.same_plane(topo.chip(c), c0)]
+    pb = [c for c in ranks if c not in pa]
+    planes = (pa, pb)
+    seq = []
+    for a in pa:
+        seq.append(a)
+        seq.extend(b for b in pb if topo.mates(topo.chip(a), topo.chip(b)))
+    groups, at = [], 0
+    for n in GROUP_SIZES:
+        groups.append(seq[at:at + n])
+        at += n
+    every = range(topo.CORES_PER_CHIP * topo.CHIPS)
+    reducers = []
+    for grp in groups:
+        for pl in (0, 1):
+            own = [c for c in grp if c in planes[pl]]
+            host = own[0] if pl == 0 else own[-1]
+            core = [c for c in every
+                    if c not in ranks and topo.chip(c) == topo.chip(host) and topo.die(c) == topo.die(host)
+                    and all(topo.may_write(c, d) for d in grp)][0]
+            def far(d, core=core):
+                a, b = topo.chip(core), topo.chip(d)
+                if a == b:
+                    return 0
+                return 1 if (topo.mates(a, b) or topo.same_plane(a, b)) else 2
+            reducers.append((core, pl, sorted(grp, key=far, reverse=True)))
+    return planes, reducers
+
+
+def _dst(topo, c):
+    rid, pid, _ = topo.addr(c)
+    return DstId(rid=rid, pnc=pid)
+
+
+def rank_program(g, core, T, topo):
+    planes, reducers = _plan(T, topo)
+    s = T.sem
+
+    if T.rank_of(core) is None:
+        mine = [r for r in reducers if r[0] == core]
+        if not mine:
+            return
+        _, pl, dsts = mine[0]
+        land = T.la if pl == 0 else T.lb
+        g.wait_ge(s.arr, PLANE * ENGINES)
+        g.remote_dma_fused(
+            [RemoteDMATransfer(dst_ids=[_dst(topo, d) for d in dsts],
+                               dma_engine_mask=_pick(_common_mask(topo, core, dsts), ENGINES),
+                               remote_sem=s.arr,
+                               srcs=[T.red[:, i * W:(i + 1) * W] for i in range(PLANE)],
+                               dsts=[land[:] for _ in dsts],
+                               alu_op=1)],
+            local_sem=s.sent)
+        g.wait_ge(s.sent, ENGINES)
+        return
+
+    pl = 0 if core in planes[0] else 1
+    slot = planes[pl].index(core)
+    reds = [r[0] for r in reducers if r[1] == pl]
+    reds.sort(key=lambda c: topo.chip(c) == topo.chip(core))
+
+    g.sync.dma_start(T.mt_s[:], T.mt[:]).then_inc(s.ld_a, 16)
+    g.scalar.dma_start(T.q_s[:], T.q[:]).then_inc(s.ld_a, 16)
+    g.scalar.dma_start(T.x[:, 0:D], T.m[:]).then_inc(s.ld_b, 16)
+
+    g.tensor.wait_ge(s.ld_a, 32)
+    g.tensor.matmul(T.ps_p[:, 0:R], T.mt_s[:], T.q_s[:], True, True).then_inc(s.mm1, 1)
+    g.vector.wait_ge(s.mm1, 1)
+    g.vector.tensor_copy(T.x[:, D:W], T.ps_p[:, 0:R]).then_inc(s.xr, 1)
+
+    g.wait_ge(s.ld_b, 16)
+    g.wait_ge(s.xr, 1)
+    g.remote_dma_fused(
+        [RemoteDMATransfer(dst_ids=[_dst(topo, c) for c in reds],
+                           dma_engine_mask=_pick(_common_mask(topo, core, reds), ENGINES),
+                           remote_sem=s.arr,
+                           srcs=[T.x[:]],
+                           dsts=[T.red[:, slot * W:(slot + 1) * W] for _ in reds],
+                           alu_op=0)],
+        local_sem=s.sent)
+
+    g.tensor.wait_ge(s.arr, 2 * ENGINES)
+    terms = [(a, b) for a in (T.la, T.lb) for b in (T.la, T.lb)]
+    for i, (a, b) in enumerate(terms):
+        mm = g.tensor.matmul(T.ps_q2[:, 0:R], a[:, 0:D], b[:, D:W], i == 0, i == len(terms) - 1)
+    mm.then_inc(s.mm2, 1)
+    g.vector.wait_ge(s.arr, 2 * ENGINES)
+    g.vector.tensor_tensor(T.p_o[:], T.la[:, D:W], T.lb[:, D:W], AluOpType.add).then_inc(s.p_r, 1)
+    g.vector.wait_ge(s.mm2, 1)
+    g.vector.tensor_copy(T.q2_o[:], T.ps_q2[:, 0:R]).then_inc(s.q2_r, 1)
+    g.scalar.wait_ge(s.p_r, 1)
+    g.scalar.dma_start(T.p[:], T.p_o[:]).then_inc(s.st, 16)
+    g.sync.wait_ge(s.q2_r, 1)
+    g.sync.dma_start(T.q2[:], T.q2_o[:]).then_inc(s.st, 16)
+    g.wait_ge(s.sent, ENGINES)
+    g.wait_ge(s.st, 32)

@@ -1,26 +1,28 @@
 from concourse.bass import DstId, RemoteDMATransfer
-from concourse.mybir import AluOpType
 
 D = 128
 R = 16
-W = D + R
 PLANE = 6
-GROUP_SIZES = (4, 4, 4)
 ENGINES = 8
+IDENT_ENGINES = 16
 
 SCRATCH = {
-    "mt_s": ("sbuf", [D, D], "bfloat16"),
+    "xd": ("dram", [D, D], "bfloat16"),
+    "red_d": ("dram", [PLANE, D, D], "bfloat16"),
+    "z": ("sbuf", [D, D + 1], "bfloat16"),
+    "zd": ("dram", [D + 1, D], "bfloat16"),
+    "ident": ("sbuf", [D, D], "bfloat16"),
     "q_s": ("sbuf", [D, R], "bfloat16"),
-    "x": ("sbuf", [D, W], "bfloat16"),
-    "red": ("sbuf", [D, PLANE * W], "bfloat16"),
-    "la": ("sbuf", [D, W], "bfloat16"),
-    "lb": ("sbuf", [D, W], "bfloat16"),
+    "la": ("sbuf", [D, D], "bfloat16"),
+    "lb": ("sbuf", [D, D], "bfloat16"),
+    "m_s": ("sbuf", [D, D], "bfloat16"),
     "p_o": ("sbuf", [D, R], "bfloat16"),
     "q2_o": ("sbuf", [D, R], "bfloat16"),
+    "ps_m": ("psum", [D, 512], "float32"),
     "ps_p": ("psum", [D, 512], "float32"),
     "ps_q2": ("psum", [D, 512], "float32"),
 }
-SEMAPHORES = ["ld_a", "ld_b", "mm1", "xr", "arr", "sent", "mm2", "p_r", "q2_r", "st"]
+SEMAPHORES = ["ld_a", "ld_b", "zs", "zl", "arr", "sent", "mm_p", "mm_m", "c_p", "c_m", "mm2", "q2_r", "st"]
 
 
 def _pick(mask, n, skip=0):
@@ -43,31 +45,14 @@ def _plan(T, topo):
     c0 = topo.chip(ranks[0])
     pa = [c for c in ranks if topo.chip(c) == c0 or topo.same_plane(topo.chip(c), c0)]
     pb = [c for c in ranks if c not in pa]
-    planes = (pa, pb)
-    seq = []
-    for a in pa:
-        seq.append(a)
-        seq.extend(b for b in pb if topo.mates(topo.chip(a), topo.chip(b)))
-    groups, at = [], 0
-    for n in GROUP_SIZES:
-        groups.append(seq[at:at + n])
-        at += n
     every = range(topo.CORES_PER_CHIP * topo.CHIPS)
-    reducers = []
-    for grp in groups:
-        for pl in (0, 1):
-            own = [c for c in grp if c in planes[pl]]
-            host = own[0] if pl == 0 else own[-1]
-            core = [c for c in every
-                    if c not in ranks and topo.chip(c) == topo.chip(host) and topo.die(c) == topo.die(host)
-                    and all(topo.may_write(c, d) for d in grp)][0]
-            def far(d, core=core):
-                a, b = topo.chip(core), topo.chip(d)
-                if a == b:
-                    return 0
-                return 1 if (topo.mates(a, b) or topo.same_plane(a, b)) else 2
-            reducers.append((core, pl, sorted(grp, key=far, reverse=True)))
-    return planes, reducers
+    mate, red = {}, {}
+    for r in ranks:
+        mate[r] = [o for o in ranks if topo.mates(topo.chip(r), topo.chip(o))][0]
+        red[r] = [c for c in every
+                  if c not in ranks and topo.chip(c) == topo.chip(r) and topo.die(c) == topo.die(r)
+                  and topo.may_write(c, mate[r])][0]
+    return (pa, pb), mate, red
 
 
 def _dst(topo, c):
@@ -75,64 +60,71 @@ def _dst(topo, c):
     return DstId(rid=rid, pnc=pid)
 
 
+def _reducer(g, core, host, T, topo, planes, mate):
+    s = T.sem
+    land = T.la if host in planes[0] else T.lb
+    g.vector.memset(T.z[:], 0.0).then_inc(s.zs, 1)
+    g.vector.wait_ge(s.zs, 1)
+    g.vector.memset(T.z[:, 0:1], 1.0).then_inc(s.zs, 1)
+    g.sync.wait_ge(s.zs, 2)
+    g.sync.dma_start(T.zd[:], T.z[:]).then_inc(s.zl, 16)
+    g.wait_ge(s.zl, 16)
+    rid, pid, _ = topo.addr(host)
+    g.remote_dma(out_ap=T.ident[:], in_ap=T.zd[0:D, :], remote_sem=s.arr, local_sem=s.sent, pid=pid, routing_id=rid,
+                 dma_engine_mask=_pick(topo.mask(core, host), IDENT_ENGINES))
+    srcs = [T.red_d[i] for i in range(PLANE)]
+    away = topo.mask(core, mate[host])
+    g.wait_ge(s.arr, PLANE * ENGINES)
+    for d, mask in ((mate[host], _pick(away, ENGINES)), (host, _pick(topo.mask(core, host) & ~away, ENGINES))):
+        g.remote_dma_fused(
+            [RemoteDMATransfer(dst_ids=[_dst(topo, d)], dma_engine_mask=mask, remote_sem=s.arr,
+                               srcs=srcs, dsts=[land[:]], alu_op=1)],
+            local_sem=s.sent)
+    g.wait_ge(s.sent, IDENT_ENGINES + 2 * ENGINES)
+
+
 def rank_program(g, core, T, topo):
-    planes, reducers = _plan(T, topo)
+    planes, mate, red = _plan(T, topo)
     s = T.sem
 
     if T.rank_of(core) is None:
-        mine = [r for r in reducers if r[0] == core]
-        if not mine:
-            return
-        _, pl, dsts = mine[0]
-        land = T.la if pl == 0 else T.lb
-        g.wait_ge(s.arr, PLANE * ENGINES)
-        g.remote_dma_fused(
-            [RemoteDMATransfer(dst_ids=[_dst(topo, d) for d in dsts],
-                               dma_engine_mask=_pick(_common_mask(topo, core, dsts), ENGINES),
-                               remote_sem=s.arr,
-                               srcs=[T.red[:, i * W:(i + 1) * W] for i in range(PLANE)],
-                               dsts=[land[:] for _ in dsts],
-                               alu_op=1)],
-            local_sem=s.sent)
-        g.wait_ge(s.sent, ENGINES)
+        for host in red:
+            if red[host] == core:
+                _reducer(g, core, host, T, topo, planes, mate)
         return
 
-    pl = 0 if core in planes[0] else 1
-    slot = planes[pl].index(core)
-    reds = [r[0] for r in reducers if r[1] == pl]
-    reds.sort(key=lambda c: topo.chip(c) == topo.chip(core))
+    plane = planes[0] if core in planes[0] else planes[1]
+    slot = plane.index(core)
+    reds = [red[plane[(slot + k) % PLANE]] for k in range(1, PLANE + 1)]
 
-    g.sync.dma_start(T.mt_s[:], T.mt[:]).then_inc(s.ld_a, 16)
-    g.scalar.dma_start(T.q_s[:], T.q[:]).then_inc(s.ld_a, 16)
-    g.scalar.dma_start(T.x[:, 0:D], T.m[:]).then_inc(s.ld_b, 16)
+    g.sync.dma_start(T.xd[:], T.mt[:]).then_inc(s.ld_a, 16)
+    g.scalar.dma_start(T.q_s[:], T.q[:]).then_inc(s.ld_b, 16)
 
-    g.tensor.wait_ge(s.ld_a, 32)
-    g.tensor.matmul(T.ps_p[:, 0:R], T.mt_s[:], T.q_s[:], True, True).then_inc(s.mm1, 1)
-    g.vector.wait_ge(s.mm1, 1)
-    g.vector.tensor_copy(T.x[:, D:W], T.ps_p[:, 0:R]).then_inc(s.xr, 1)
-
-    g.wait_ge(s.ld_b, 16)
-    g.wait_ge(s.xr, 1)
+    g.wait_ge(s.ld_a, 16)
     g.remote_dma_fused(
         [RemoteDMATransfer(dst_ids=[_dst(topo, c) for c in reds],
                            dma_engine_mask=_pick(_common_mask(topo, core, reds), ENGINES),
-                           remote_sem=s.arr,
-                           srcs=[T.x[:]],
-                           dsts=[T.red[:, slot * W:(slot + 1) * W] for _ in reds],
-                           alu_op=0)],
+                           remote_sem=s.arr, srcs=[T.xd[:]], dsts=[T.red_d[slot] for _ in reds], alu_op=0)],
         local_sem=s.sent)
 
-    g.tensor.wait_ge(s.arr, 2 * ENGINES)
-    terms = [(a, b) for a in (T.la, T.lb) for b in (T.la, T.lb)]
-    for i, (a, b) in enumerate(terms):
-        mm = g.tensor.matmul(T.ps_q2[:, 0:R], a[:, 0:D], b[:, D:W], i == 0, i == len(terms) - 1)
-    mm.then_inc(s.mm2, 1)
-    g.vector.wait_ge(s.arr, 2 * ENGINES)
-    g.vector.tensor_tensor(T.p_o[:], T.la[:, D:W], T.lb[:, D:W], AluOpType.add).then_inc(s.p_r, 1)
+    due = IDENT_ENGINES + 2 * ENGINES
+    g.tensor.wait_ge(s.ld_b, 16)
+    g.tensor.wait_ge(s.arr, due)
+    g.tensor.matmul(T.ps_p[:, 0:R], T.la[:], T.q_s[:], True, False)
+    g.tensor.matmul(T.ps_p[:, 0:R], T.lb[:], T.q_s[:], False, True).then_inc(s.mm_p, 1)
+    g.tensor.matmul(T.ps_m[:, 0:D], T.la[:], T.ident[:], True, False)
+    g.tensor.matmul(T.ps_m[:, 0:D], T.lb[:], T.ident[:], False, True).then_inc(s.mm_m, 1)
+    g.vector.wait_ge(s.mm_p, 1)
+    g.vector.tensor_copy(T.p_o[:], T.ps_p[:, 0:R]).then_inc(s.c_p, 1)
+    g.vector.wait_ge(s.mm_m, 1)
+    g.vector.tensor_copy(T.m_s[:], T.ps_m[:, 0:D]).then_inc(s.c_m, 1)
+    g.scalar.wait_ge(s.c_p, 1)
+    g.scalar.dma_start(T.p[:], T.p_o[:]).then_inc(s.st, 16)
+    g.tensor.wait_ge(s.c_p, 1)
+    g.tensor.wait_ge(s.c_m, 1)
+    g.tensor.matmul(T.ps_q2[:, 0:R], T.m_s[:], T.p_o[:], True, True).then_inc(s.mm2, 1)
     g.vector.wait_ge(s.mm2, 1)
     g.vector.tensor_copy(T.q2_o[:], T.ps_q2[:, 0:R]).then_inc(s.q2_r, 1)
-    g.scalar.wait_ge(s.p_r, 1)
-    g.scalar.dma_start(T.p[:], T.p_o[:]).then_inc(s.st, 16)
     g.sync.wait_ge(s.q2_r, 1)
     g.sync.dma_start(T.q2[:], T.q2_o[:]).then_inc(s.st, 16)
     g.wait_ge(s.sent, ENGINES)

@@ -1,28 +1,32 @@
 from concourse.bass import DstId, RemoteDMATransfer
+from concourse.mybir import AluOpType
 
 D = 128
+H = 64
 R = 16
 PLANE = 6
 ENGINES = 8
-IDENT_ENGINES = 16
+CHIP_ENGINES = 16
 
 SCRATCH = {
     "xd": ("dram", [D, D], "bfloat16"),
     "red_d": ("dram", [PLANE, D, D], "bfloat16"),
-    "z": ("sbuf", [D, D + 1], "bfloat16"),
-    "zd": ("dram", [D + 1, D], "bfloat16"),
-    "ident": ("sbuf", [D, D], "bfloat16"),
+    "ones": ("sbuf", [D, H], "bfloat16"),
+    "ones_in": ("sbuf", [D, H], "bfloat16"),
+    "idl": ("sbuf", [D, H], "bfloat16"),
+    "idr": ("sbuf", [D, H], "bfloat16"),
     "q_s": ("sbuf", [D, R], "bfloat16"),
     "la": ("sbuf", [D, D], "bfloat16"),
     "lb": ("sbuf", [D, D], "bfloat16"),
     "m_s": ("sbuf", [D, D], "bfloat16"),
     "p_o": ("sbuf", [D, R], "bfloat16"),
     "q2_o": ("sbuf", [D, R], "bfloat16"),
-    "ps_m": ("psum", [D, 512], "float32"),
+    "ps_ml": ("psum", [D, 512], "float32"),
+    "ps_mr": ("psum", [D, 512], "float32"),
     "ps_p": ("psum", [D, 512], "float32"),
     "ps_q2": ("psum", [D, 512], "float32"),
 }
-SEMAPHORES = ["ld_a", "ld_b", "zs", "zl", "arr", "sent", "mm_p", "mm_m", "c_p", "c_m", "mm2", "q2_r", "st"]
+SEMAPHORES = ["ld_a", "ld_b", "zs", "oa", "arr", "sent", "mm_p", "mm_l", "mm_r", "c_p", "c_m", "mm2", "q2_r", "st"]
 
 
 def _pick(mask, n, skip=0):
@@ -63,15 +67,19 @@ def _dst(topo, c):
 def _reducer(g, core, host, T, topo, planes, mate):
     s = T.sem
     land = T.la if host in planes[0] else T.lb
-    g.vector.memset(T.z[:], 0.0).then_inc(s.zs, 1)
-    g.vector.wait_ge(s.zs, 1)
-    g.vector.memset(T.z[:, 0:1], 1.0).then_inc(s.zs, 1)
-    g.sync.wait_ge(s.zs, 2)
-    g.sync.dma_start(T.zd[:], T.z[:]).then_inc(s.zl, 16)
-    g.wait_ge(s.zl, 16)
     rid, pid, _ = topo.addr(host)
-    g.remote_dma(out_ap=T.ident[:], in_ap=T.zd[0:D, :], remote_sem=s.arr, local_sem=s.sent, pid=pid, routing_id=rid,
-                 dma_engine_mask=_pick(topo.mask(core, host), IDENT_ENGINES))
+    chip_mask = _pick(topo.mask(core, host), CHIP_ENGINES)
+    g.vector.memset(T.ones[:], 1.0).then_inc(s.zs, 1)
+    g.wait_ge(s.zs, 1)
+    g.affine_select(T.ones[:], T.ones[:], [[-1, H]], AluOpType.is_equal, 0.0, 0, 1).then_inc(s.zs, 1)
+    g.wait_ge(s.zs, 2)
+    g.remote_dma(out_ap=T.idl[:], in_ap=T.ones[:], remote_sem=s.arr, local_sem=s.sent, pid=pid, routing_id=rid,
+                 dma_engine_mask=chip_mask)
+    g.wait_ge(s.oa, CHIP_ENGINES)
+    g.affine_select(T.ones_in[:], T.ones_in[:], [[-1, H]], AluOpType.is_equal, 0.0, -H, 1).then_inc(s.zs, 1)
+    g.wait_ge(s.zs, 3)
+    g.remote_dma(out_ap=T.idr[:], in_ap=T.ones_in[:], remote_sem=s.arr, local_sem=s.sent, pid=pid, routing_id=rid,
+                 dma_engine_mask=chip_mask)
     srcs = [T.red_d[i] for i in range(PLANE)]
     away = topo.mask(core, mate[host])
     g.wait_ge(s.arr, PLANE * ENGINES)
@@ -80,7 +88,7 @@ def _reducer(g, core, host, T, topo, planes, mate):
             [RemoteDMATransfer(dst_ids=[_dst(topo, d)], dma_engine_mask=mask, remote_sem=s.arr,
                                srcs=srcs, dsts=[land[:]], alu_op=1)],
             local_sem=s.sent)
-    g.wait_ge(s.sent, IDENT_ENGINES + 2 * ENGINES)
+    g.wait_ge(s.sent, 2 * CHIP_ENGINES + 2 * ENGINES)
 
 
 def rank_program(g, core, T, topo):
@@ -100,6 +108,12 @@ def rank_program(g, core, T, topo):
     g.sync.dma_start(T.xd[:], T.mt[:]).then_inc(s.ld_a, 16)
     g.scalar.dma_start(T.q_s[:], T.q[:]).then_inc(s.ld_b, 16)
 
+    g.vector.memset(T.ones[:], 1.0).then_inc(s.zs, 1)
+    g.wait_ge(s.zs, 1)
+    rid, pid, _ = topo.addr(red[core])
+    g.remote_dma(out_ap=T.ones_in[:], in_ap=T.ones[:], remote_sem=s.oa, local_sem=s.sent, pid=pid, routing_id=rid,
+                 dma_engine_mask=_pick(topo.mask(core, red[core]), CHIP_ENGINES))
+
     g.wait_ge(s.ld_a, 16)
     g.remote_dma_fused(
         [RemoteDMATransfer(dst_ids=[_dst(topo, c) for c in reds],
@@ -107,25 +121,29 @@ def rank_program(g, core, T, topo):
                            remote_sem=s.arr, srcs=[T.xd[:]], dsts=[T.red_d[slot] for _ in reds], alu_op=0)],
         local_sem=s.sent)
 
-    due = IDENT_ENGINES + 2 * ENGINES
+    due = 2 * CHIP_ENGINES + 2 * ENGINES
     g.tensor.wait_ge(s.ld_b, 16)
     g.tensor.wait_ge(s.arr, due)
     g.tensor.matmul(T.ps_p[:, 0:R], T.la[:], T.q_s[:], True, False)
     g.tensor.matmul(T.ps_p[:, 0:R], T.lb[:], T.q_s[:], False, True).then_inc(s.mm_p, 1)
-    g.tensor.matmul(T.ps_m[:, 0:D], T.la[:], T.ident[:], True, False)
-    g.tensor.matmul(T.ps_m[:, 0:D], T.lb[:], T.ident[:], False, True).then_inc(s.mm_m, 1)
+    g.tensor.matmul(T.ps_ml[:, 0:H], T.la[:], T.idl[:], True, False)
+    g.tensor.matmul(T.ps_ml[:, 0:H], T.lb[:], T.idl[:], False, True).then_inc(s.mm_l, 1)
+    g.tensor.matmul(T.ps_mr[:, 0:H], T.la[:], T.idr[:], True, False)
+    g.tensor.matmul(T.ps_mr[:, 0:H], T.lb[:], T.idr[:], False, True).then_inc(s.mm_r, 1)
     g.vector.wait_ge(s.mm_p, 1)
     g.vector.tensor_copy(T.p_o[:], T.ps_p[:, 0:R]).then_inc(s.c_p, 1)
-    g.vector.wait_ge(s.mm_m, 1)
-    g.vector.tensor_copy(T.m_s[:], T.ps_m[:, 0:D]).then_inc(s.c_m, 1)
+    g.vector.wait_ge(s.mm_l, 1)
+    g.vector.tensor_copy(T.m_s[:, 0:H], T.ps_ml[:, 0:H]).then_inc(s.c_m, 1)
+    g.vector.wait_ge(s.mm_r, 1)
+    g.vector.tensor_copy(T.m_s[:, H:D], T.ps_mr[:, 0:H]).then_inc(s.c_m, 1)
     g.scalar.wait_ge(s.c_p, 1)
     g.scalar.dma_start(T.p[:], T.p_o[:]).then_inc(s.st, 16)
     g.tensor.wait_ge(s.c_p, 1)
-    g.tensor.wait_ge(s.c_m, 1)
+    g.tensor.wait_ge(s.c_m, 2)
     g.tensor.matmul(T.ps_q2[:, 0:R], T.m_s[:], T.p_o[:], True, True).then_inc(s.mm2, 1)
     g.vector.wait_ge(s.mm2, 1)
     g.vector.tensor_copy(T.q2_o[:], T.ps_q2[:, 0:R]).then_inc(s.q2_r, 1)
     g.sync.wait_ge(s.q2_r, 1)
     g.sync.dma_start(T.q2[:], T.q2_o[:]).then_inc(s.st, 16)
-    g.wait_ge(s.sent, ENGINES)
+    g.wait_ge(s.sent, CHIP_ENGINES + ENGINES)
     g.wait_ge(s.st, 32)

from concourse.bass import DstId, RemoteDMATransfer
from concourse.mybir import AluOpType

D = 128
H = 64
R = 16
PLANE = 6
ENGINES = 8
CHIP_ENGINES = 16

SCRATCH = {
    "xd": ("dram", [D, D], "bfloat16"),
    "red_d": ("dram", [PLANE, D, D], "bfloat16"),
    "ones": ("sbuf", [D, H], "bfloat16"),
    "ones_in": ("sbuf", [D, H], "bfloat16"),
    "idl": ("sbuf", [D, H], "bfloat16"),
    "idr": ("sbuf", [D, H], "bfloat16"),
    "q_s": ("sbuf", [D, R], "bfloat16"),
    "la": ("sbuf", [D, D], "bfloat16"),
    "lb": ("sbuf", [D, D], "bfloat16"),
    "m_s": ("sbuf", [D, D], "bfloat16"),
    "p_o": ("sbuf", [D, R], "bfloat16"),
    "q2_o": ("sbuf", [D, R], "bfloat16"),
    "ps_ml": ("psum", [D, 512], "float32"),
    "ps_mr": ("psum", [D, 512], "float32"),
    "ps_p": ("psum", [D, 512], "float32"),
    "ps_q2": ("psum", [D, 512], "float32"),
}
SEMAPHORES = ["ld_a", "ld_b", "zs", "oa", "arr", "sent", "mm_p", "mm_l", "mm_r", "c_p", "c_m", "mm2", "q2_r", "st"]


def _pick(mask, n, skip=0):
    bits = [b for b in range(mask.bit_length()) if (mask >> b) & 1]
    out = 0
    for b in bits[skip:skip + n]:
        out |= 1 << b
    return out


def _common_mask(topo, src, dsts):
    m = topo.mask(src, dsts[0])
    for d in dsts[1:]:
        m &= topo.mask(src, d)
    return m


def _plan(T, topo):
    ranks = list(T.cores)
    c0 = topo.chip(ranks[0])
    pa = [c for c in ranks if topo.chip(c) == c0 or topo.same_plane(topo.chip(c), c0)]
    pb = [c for c in ranks if c not in pa]
    every = range(topo.CORES_PER_CHIP * topo.CHIPS)
    mate, red = {}, {}
    for r in ranks:
        mate[r] = [o for o in ranks if topo.mates(topo.chip(r), topo.chip(o))][0]
        red[r] = [c for c in every
                  if c not in ranks and topo.chip(c) == topo.chip(r) and topo.die(c) == topo.die(r)
                  and topo.may_write(c, mate[r])][0]
    return (pa, pb), mate, red


def _dst(topo, c):
    rid, pid, _ = topo.addr(c)
    return DstId(rid=rid, pnc=pid)


def _reducer(g, core, host, T, topo, planes, mate):
    s = T.sem
    land = T.la if host in planes[0] else T.lb
    rid, pid, _ = topo.addr(host)
    chip_mask = _pick(topo.mask(core, host), CHIP_ENGINES)
    g.vector.memset(T.ones[:], 1.0).then_inc(s.zs, 1)
    g.wait_ge(s.zs, 1)
    g.affine_select(T.ones[:], T.ones[:], [[-1, H]], AluOpType.is_equal, 0.0, 0, 1).then_inc(s.zs, 1)
    g.wait_ge(s.zs, 2)
    g.remote_dma(out_ap=T.idl[:], in_ap=T.ones[:], remote_sem=s.arr, local_sem=s.sent, pid=pid, routing_id=rid,
                 dma_engine_mask=chip_mask)
    g.wait_ge(s.oa, CHIP_ENGINES)
    g.affine_select(T.ones_in[:], T.ones_in[:], [[-1, H]], AluOpType.is_equal, 0.0, -H, 1).then_inc(s.zs, 1)
    g.wait_ge(s.zs, 3)
    g.remote_dma(out_ap=T.idr[:], in_ap=T.ones_in[:], remote_sem=s.arr, local_sem=s.sent, pid=pid, routing_id=rid,
                 dma_engine_mask=chip_mask)
    srcs = [T.red_d[i] for i in range(PLANE)]
    away = topo.mask(core, mate[host])
    g.wait_ge(s.arr, PLANE * ENGINES)
    for d, mask in ((mate[host], _pick(away, ENGINES)), (host, _pick(topo.mask(core, host) & ~away, ENGINES))):
        g.remote_dma_fused(
            [RemoteDMATransfer(dst_ids=[_dst(topo, d)], dma_engine_mask=mask, remote_sem=s.arr,
                               srcs=srcs, dsts=[land[:]], alu_op=1)],
            local_sem=s.sent)
    g.wait_ge(s.sent, 2 * CHIP_ENGINES + 2 * ENGINES)


def rank_program(g, core, T, topo):
    planes, mate, red = _plan(T, topo)
    s = T.sem

    if T.rank_of(core) is None:
        for host in red:
            if red[host] == core:
                _reducer(g, core, host, T, topo, planes, mate)
        return

    plane = planes[0] if core in planes[0] else planes[1]
    slot = plane.index(core)
    reds = [red[plane[(slot + k) % PLANE]] for k in range(1, PLANE + 1)]

    g.sync.dma_start(T.xd[:], T.mt[:]).then_inc(s.ld_a, 16)
    g.scalar.dma_start(T.q_s[:], T.q[:]).then_inc(s.ld_b, 16)

    g.vector.memset(T.ones[:], 1.0).then_inc(s.zs, 1)
    g.wait_ge(s.zs, 1)
    rid, pid, _ = topo.addr(red[core])
    g.remote_dma(out_ap=T.ones_in[:], in_ap=T.ones[:], remote_sem=s.oa, local_sem=s.sent, pid=pid, routing_id=rid,
                 dma_engine_mask=_pick(topo.mask(core, red[core]), CHIP_ENGINES))

    g.wait_ge(s.ld_a, 16)
    g.remote_dma_fused(
        [RemoteDMATransfer(dst_ids=[_dst(topo, c) for c in reds],
                           dma_engine_mask=_pick(_common_mask(topo, core, reds), ENGINES),
                           remote_sem=s.arr, srcs=[T.xd[:]], dsts=[T.red_d[slot] for _ in reds], alu_op=0)],
        local_sem=s.sent)

    due = 2 * CHIP_ENGINES + 2 * ENGINES
    g.tensor.wait_ge(s.ld_b, 16)
    g.tensor.wait_ge(s.arr, due)
    g.tensor.matmul(T.ps_p[:, 0:R], T.la[:], T.q_s[:], True, False)
    g.tensor.matmul(T.ps_p[:, 0:R], T.lb[:], T.q_s[:], False, True).then_inc(s.mm_p, 1)
    g.tensor.matmul(T.ps_ml[:, 0:H], T.la[:], T.idl[:], True, False)
    g.tensor.matmul(T.ps_ml[:, 0:H], T.lb[:], T.idl[:], False, True).then_inc(s.mm_l, 1)
    g.tensor.matmul(T.ps_mr[:, 0:H], T.la[:], T.idr[:], True, False)
    g.tensor.matmul(T.ps_mr[:, 0:H], T.lb[:], T.idr[:], False, True).then_inc(s.mm_r, 1)
    g.vector.wait_ge(s.mm_p, 1)
    g.vector.tensor_copy(T.p_o[:], T.ps_p[:, 0:R]).then_inc(s.c_p, 1)
    g.vector.wait_ge(s.mm_l, 1)
    g.vector.tensor_copy(T.m_s[:, 0:H], T.ps_ml[:, 0:H]).then_inc(s.c_m, 1)
    g.vector.wait_ge(s.mm_r, 1)
    g.vector.tensor_copy(T.m_s[:, H:D], T.ps_mr[:, 0:H]).then_inc(s.c_m, 1)
    g.scalar.wait_ge(s.c_p, 1)
    g.scalar.dma_start(T.p[:], T.p_o[:]).then_inc(s.st, 16)
    g.tensor.wait_ge(s.c_p, 1)
    g.tensor.wait_ge(s.c_m, 2)
    g.tensor.matmul(T.ps_q2[:, 0:R], T.m_s[:], T.p_o[:], True, True).then_inc(s.mm2, 1)
    g.vector.wait_ge(s.mm2, 1)
    g.vector.tensor_copy(T.q2_o[:], T.ps_q2[:, 0:R]).then_inc(s.q2_r, 1)
    g.sync.wait_ge(s.q2_r, 1)
    g.sync.dma_start(T.q2[:], T.q2_o[:]).then_inc(s.st, 16)
    g.wait_ge(s.sent, CHIP_ENGINES + ENGINES)
    g.wait_ge(s.st, 32)
